import numpy as np
import ml_dtypes


def mxq(x, axis, fmt="e4m3"):
    dtype, down = {"e4m3": (ml_dtypes.float8_e4m3fn, 7), "e5m2": (ml_dtypes.float8_e5m2, 14)}[fmt]
    v = np.moveaxis(np.asarray(x, np.float32).astype(ml_dtypes.bfloat16).astype(np.float64), axis, -1)
    blocks = v.reshape(v.shape[:-1] + (-1, 32))
    amax = np.abs(blocks).max(-1, keepdims=True)
    byte = np.maximum(np.where(amax > 0, np.frexp(amax)[1] - 1 + 127, 0) - down, 1)
    scale = np.exp2(byte - 127.0)
    codes = (blocks / scale).astype(np.float32).astype(dtype).astype(np.float64)
    return np.moveaxis((codes * scale).reshape(v.shape), -1, axis)


WIDE = False


def mx_kscale(k):
    if not WIDE:
        return np.ones(k)
    levels = np.array([10, -10, 5, -5, 0])
    if k % 512:
        return np.exp2(np.random.permutation(np.resize(levels, k // 32))).repeat(32)
    a = np.empty((k // 512, 16))
    for p in range(k // 512):
        a[p, :8] = np.random.permutation(np.resize(levels, 8))
        for g in range(8):
            far = levels[np.abs(levels - a[p, g]) >= 10]
            a[p, g + 8] = far[np.random.randint(len(far))]
    return np.exp2(a.ravel()).repeat(32)


def f64(x):
    return np.asarray(x).astype(np.float64)


def striped(idx):
    return np.tile(idx.reshape(-1, 16).T, (8, 1)).astype(np.uint16)


def unstriped(offs):
    return offs[:16].T.reshape(-1).astype(np.int64)


E2M1 = np.array([0.0, 0.5, 1.0, 1.5, 2.0, 3.0, 4.0, 6.0, -0.0, -0.5, -1.0, -1.5, -2.0, -3.0, -4.0, -6.0])


def pack_weight(w, fmt):
    k, n = w.shape
    w = f64(np.asarray(w, np.float32).astype(ml_dtypes.bfloat16)).reshape(k // 32, 32, n)
    amax = np.abs(w).max(1)
    if fmt == "e4m3":
        byte = np.frexp(amax)[1] - 1 + 127 - 7
    else:
        mant, ex = np.frexp(amax / 6.0)
        byte = np.where(mant > 0.5, ex, ex - 1) + 127
    byte = np.clip(np.where(amax > 0, byte, 1), 1, 254)
    scaled = (w * np.exp2(127.0 - byte)[:, None, :]).reshape(k, n).astype(np.float32)
    by_word = np.ascontiguousarray(scaled.reshape(k // 512, 128, 4, n).transpose(0, 1, 3, 2))
    if fmt == "e4m3":
        words = by_word.astype(ml_dtypes.float8_e4m3fn).view(np.uint8)
    else:
        c = by_word.astype(ml_dtypes.float4_e2m1fn).view(np.uint8) & 0xF
        words = (c[..., 0::2] | (c[..., 1::2] << 4)).reshape(k // 512, 128, 2 * n)
    return np.ascontiguousarray(words), np.ascontiguousarray(byte.astype(np.uint8).reshape(k // 512, 16, n))


def unpack_weight(words, scales, fmt):
    g, _, n = scales.shape
    words = np.ascontiguousarray(words).reshape(g, 128, n, -1)
    if fmt == "e4m3":
        vals = words.view(ml_dtypes.float8_e4m3fn).astype(np.float64)
    else:
        nib = np.empty((g, 128, n, 4), np.uint8)
        nib[..., 0::2] = words & 0xF
        nib[..., 1::2] = words >> 4
        vals = E2M1[nib]
    vals = vals * np.repeat(np.exp2(scales.astype(np.float64) - 127.0), 8, axis=1)[..., None]
    return vals.transpose(0, 1, 3, 2).reshape(g * 512, n)


def gelu(v):
    return 0.5 * v * (1.0 + np.tanh(np.sqrt(2.0 / np.pi) * (v + 0.044715 * v**3)))


K, T, E, C, H, N = 2048, 640, 4, 128, 512, 512


def by_expert(wq, xq):
    return np.concatenate([wq[e].T @ xq[:, e * C:(e + 1) * C] for e in range(E)], axis=1)


def setup_inputs():
    n = np.random.standard_normal
    s = mx_kscale(K)[:, None]
    u = mx_kscale(H)
    w1 = [pack_weight(m, "e2m1") for m in n((E, K, H)) / np.sqrt(K) / s[None] * u[None, None, :]]
    w2 = [pack_weight(m, "e2m1") for m in n((E, H, N)) / np.sqrt(H) / u[None, :, None]]
    return {
        "xT": (n((K, T)) * s).astype(np.float32),
        "w1_words": np.stack([m[0] for m in w1]),
        "w1_scales": np.stack([m[1] for m in w1]),
        "w2_words": np.stack([m[0] for m in w2]),
        "w2_scales": np.stack([m[1] for m in w2]),
        "gate": np.tile(np.random.uniform(0.2, 1.0, E * C), (K, 1)).astype(np.float32),
        "offs": striped(np.random.permutation(T)[:E * C]),
    }


def reference(xT, w1_words, w1_scales, w2_words, w2_scales, gate, offs):
    idx = unstriped(offs)
    w1 = np.stack([unpack_weight(w1_words[e], w1_scales[e], "e2m1") for e in range(E)])
    w2 = np.stack([unpack_weight(w2_words[e], w2_scales[e], "e2m1") for e in range(E)])
    xq = mxq(f64(gate) * f64(xT)[:, idx], 0, "e4m3")
    h = gelu(by_expert(w1, xq))
    y = by_expert(w2, mxq(h, 0, "e4m3"))
    out = np.zeros((N, T))
    out[:, idx] = y
    return out

@@ -1,0 +1,225 @@
+from contextlib import ExitStack
+
+import concourse.mybir as mybir
+from concourse.masks import make_identity
+
+K, T, E, C, H, N = 2048, 640, 4, 128, 512, 512
+S = E * C
+P = 128
+PACK = 4
+K_PASS = P * PACK
+PASSES = K // K_PASS
+N_TILES = N // P
+
+FLOPS = 2 * S * (K * H + H * N)
+BYTES = 4 * K * T + E * (K * H + H * N) // 2 + E * (K * H + H * N) // 32 + 4 * P * S + 2 * P * S // 16 + 4 * N * T
+
+F32 = mybir.dt.float32
+BF16 = mybir.dt.bfloat16
+I32 = mybir.dt.int32
+U32 = mybir.dt.uint32
+U16 = mybir.dt.uint16
+U8 = mybir.dt.uint8
+FP8X4 = mybir.dt.float8_e4m3fn_x4
+FP4X4 = mybir.dt.float4_e2m1fn_x4
+MULT = mybir.AluOpType.mult
+GELU = mybir.ActivationFunctionType.Gelu_apprx_tanh
+
+
+def tile_moe_pre_mlp_gelu_kernel(
+    tc, xT, w1_words, w1_scales, w2_words, w2_scales, gate, offs, out
+):
+    nc = tc.nc
+    with ExitStack() as ctx:
+        keep = ctx.enter_context(tc.tile_pool(name="keep", bufs=1))
+        ring = ctx.enter_context(tc.tile_pool(name="ring", bufs=2))
+        psum = ctx.enter_context(tc.psum_pool(name="psum", bufs=1))
+
+        offsets = keep.tile([P, S // 16], U16, name="offsets")
+        gate_sb = keep.tile([P, S], F32, name="gate_sb")
+        x_rows = [[keep.tile([P, T], F32, name=f"x{s}_{t}") for t in range(PACK)] for s in range(PASSES)]
+        w1 = [keep.tile([P, PASSES, 2 * H], U8, name=f"w1_{e}", align_bytes=64) for e in range(E)]
+        w2 = [keep.tile([P, 2 * N], U8, name=f"w2_{e}", align_bytes=64) for e in range(E)]
+        w1s = [keep.tile([P, 2, PASSES, H], U8, name=f"w1s_{g}", align_bytes=64) for g in range(2)]
+        w2s = keep.tile([P, E, N], U8, name="w2s", align_bytes=64)
+        ident = keep.tile([P, P], F32, name="ident")
+        windows = [keep.tile([P, T], F32, name=f"win{j}") for j in range(N_TILES)]
+        x_bf = [keep.tile([P, S, PACK], BF16, name=f"xb{s}", align_bytes=64) for s in range(PASSES)]
+        x_codes = [keep.tile([P, S], U32, name=f"xq{s}", align_bytes=64) for s in range(PASSES)]
+        x_scales = [keep.tile([P, S], U8, name=f"xs{s}", align_bytes=64) for s in range(PASSES)]
+        h_slot = [keep.tile([P, H], BF16, name=f"hs{e}", align_bytes=64) for e in range(E)]
+        h_bf = [keep.tile([P, C * PACK], BF16, name=f"hb{e}", align_bytes=64) for e in range(E)]
+        h_codes = [keep.tile([P, C], U32, name=f"hq{e}", align_bytes=64) for e in range(E)]
+        h_scales = [keep.tile([P, C], U8, name=f"hsc{e}", align_bytes=64) for e in range(E)]
+        y_sb = keep.tile([P, N_TILES, S], F32, name="y_sb")
+        a_ps = [psum.tile([P, H], F32, name=f"a{e}") for e in range(E)]
+        t_ps = [psum.tile([P, 2, C], F32, name=f"t{j}") for j in range(2)]
+        y_ps = [psum.tile([P, N_TILES, C], F32, name=f"y{j}") for j in range(2)]
+
+        def load_x(s, t):
+            rows = xT[s * K_PASS : (s + 1) * K_PASS, :].rearrange("(p t) c -> t p c", t=PACK)
+            nc.sync.dma_start(out=x_rows[s][t][:], in_=rows[t])
+
+        def load_w1(e):
+            nc.sync.dma_start(out=w1[e][:].bitcast(I32), in_=w1_words[e].rearrange("s p b -> p s b").bitcast(I32))
+
+        def load_w2(e):
+            nc.sync.dma_start(out=w2[e][:].bitcast(I32), in_=w2_words[e, 0].bitcast(I32))
+
+        def load_w1_scales(g):
+            src = w1_scales[2 * g : 2 * g + 2].rearrange("e s q i -> q (e s) i")
+            dst = w1s[g][:].rearrange("p e s i -> p (e s) i")
+            for quad in range(4):
+                nc.sync.dma_start(
+                    out=dst[32 * quad : 32 * quad + 4].bitcast(I32), in_=src[4 * quad : 4 * quad + 4].bitcast(I32)
+                )
+
+        def load_w2_scales():
+            src = w2_scales.rearrange("e s q n -> q (e s) n")
+            for quad in range(4):
+                nc.sync.dma_start(
+                    out=w2s[32 * quad : 32 * quad + 4].bitcast(I32), in_=src[4 * quad : 4 * quad + 4].bitcast(I32)
+                )
+
+        def gather(s, c0, c1):
+            gathered = ring.tile([P, PACK, c1 - c0], F32, name="gathered")
+            for t in range(PACK):
+                nc.vector.tensor_tensor(
+                    gathered[:, t, :],
+                    x_rows[s][t][:].indirect(offsets[:, c0 // 16 : c1 // 16]),
+                    gate_sb[:, c0:c1],
+                    MULT,
+                )
+            nc.scalar.copy(
+                out=x_bf[s][:, c0:c1, :].rearrange("p (c i) t -> p c t i", i=4),
+                in_=gathered[:].rearrange("p t (c i) -> p c t i", i=4),
+            )
+
+        def quantize_x(s, c0, c1):
+            nc.vector.quantize_mx(
+                out=x_codes[s][:, c0:c1].bitcast(FP8X4),
+                scales=x_scales[s][:, c0:c1],
+                in_=x_bf[s][:, c0:c1, :].rearrange("p c t -> p (c t)"),
+            )
+
+        def layer1(e, s):
+            cols = slice(e * C, (e + 1) * C)
+            nc.tensor.matmul_mx(
+                out=a_ps[e][:],
+                lhsT=x_codes[s][:, cols].bitcast(FP8X4),
+                lhsT_scale=x_scales[s][:, cols],
+                rhs=w1[e][:, s, :].bitcast(FP4X4),
+                rhs_scale=w1s[e // 2][:, e % 2, s, :],
+                start=(s == 0),
+                stop=(s == PASSES - 1),
+            )
+
+        def hidden(e):
+            nc.scalar.activation(
+                out=h_slot[e][:].rearrange("c (u m d) -> c u m d", u=2, d=2),
+                in_=a_ps[e][:].rearrange("c (m u d) -> c u m d", u=2, d=2),
+                func=GELU,
+            )
+            words = h_slot[e][:].bitcast(F32)
+            tp = t_ps[e % 2]
+            for u in range(2):
+                nc.tensor.transpose(tp[:, u, :], words[:, u * P : (u + 1) * P], ident[:])
+            nc.scalar.copy(
+                out=h_bf[e][:].bitcast(F32).rearrange("p (c u) -> p c u", u=2),
+                in_=tp[:].rearrange("p u c -> p c u"),
+            )
+
+        def layer2(e):
+            nc.vector.quantize_mx(out=h_codes[e][:].bitcast(FP8X4), scales=h_scales[e][:], in_=h_bf[e][:])
+            yp = y_ps[e % 2]
+            for j in range(N_TILES):
+                nc.tensor.matmul_mx(
+                    out=yp[:, j, :],
+                    lhsT=w2[e][:, 2 * j * P : 2 * (j + 1) * P].bitcast(FP4X4),
+                    lhsT_scale=w2s[:, e, j * P : (j + 1) * P],
+                    rhs=h_codes[e][:].bitcast(FP8X4),
+                    rhs_scale=h_scales[e][:],
+                    start=True,
+                    stop=True,
+                )
+            nc.scalar.copy(out=y_sb[:, :, e * C : (e + 1) * C], in_=yp[:])
+
+        def scatter(j, c0, c1):
+            nc.vector.tensor_copy(windows[j][:].indirect(offsets[:, c0 // 16 : c1 // 16]), y_sb[:, j, c0:c1])
+
+        for g in range(2):
+            nc.vector.memset(w1s[g][:].rearrange("p e s i -> p (e s i)").bitcast(I32), 0)
+        nc.vector.memset(w2s[:].rearrange("p e n -> p (e n)").bitcast(I32), 0)
+        nc.vector.memset(windows[0][:], 0.0)
+        for j in range(1, N_TILES):
+            nc.scalar.activation(out=windows[j][:], in_=windows[0][:], func=GELU)
+        make_identity(nc, ident[:])
+
+        nc.sync.dma_start(offsets[:], offs)
+        load_x(0, 0)
+        nc.sync.dma_start(out=gate_sb[:], in_=gate[0:P, :])
+        for s in range(2):
+            for t in range(PACK):
+                if (s, t) != (0, 0):
+                    load_x(s, t)
+        load_w1_scales(0)
+        for s in range(2, PASSES):
+            for t in range(PACK):
+                load_x(s, t)
+        load_w1(0)
+        load_w1(1)
+        load_w2_scales()
+        load_w1_scales(1)
+        load_w2(0)
+        load_w2(1)
+        load_w1(2)
+        load_w1(3)
+        load_w2(2)
+        load_w2(3)
+
+        gather(0, 0, S)
+        gather(1, 0, S)
+        quantize_x(0, 0, S)
+        gather(2, 0, 2 * C)
+        quantize_x(1, 0, S)
+        gather(3, 0, C)
+        quantize_x(2, 0, 2 * C)
+        for s in range(3):
+            layer1(0, s)
+        gather(3, C, 2 * C)
+        quantize_x(3, 0, C)
+        layer1(0, 3)
+        hidden(0)
+        for s in range(3):
+            layer1(1, s)
+        gather(2, 2 * C, S)
+        quantize_x(3, C, 2 * C)
+        layer1(1, 3)
+        hidden(1)
+        gather(3, 2 * C, 3 * C)
+        layer2(0)
+        quantize_x(2, 2 * C, S)
+        for s in range(3):
+            layer1(2, s)
+        gather(3, 3 * C, S)
+        quantize_x(3, 2 * C, 3 * C)
+        layer1(2, 3)
+        hidden(2)
+        layer2(1)
+        for s in range(3):
+            layer1(3, s)
+        scatter(0, 0, C)
+        quantize_x(3, 3 * C, S)
+        layer1(3, 3)
+        hidden(3)
+        for j in range(1, N_TILES):
+            scatter(j, 0, C)
+        layer2(2)
+        for j in range(N_TILES):
+            scatter(j, C, 2 * C)
+        layer2(3)
+        for j in range(N_TILES):
+            scatter(j, 2 * C, 3 * C)
+        for j in range(N_TILES):
+            scatter(j, 3 * C, S)
+            nc.sync.dma_start(out=out[j * P : (j + 1) * P, :], in_=windows[j][:])

@@ -5,6 +5,7 @@ from concourse.masks import make_identity
 
 K, T, E, C, H, N = 2048, 640, 4, 128, 512, 512
 S = E * C
+G = 2 * C
 P = 128
 PACK = 4
 K_PASS = P * PACK
@@ -32,29 +33,23 @@ def tile_moe_pre_mlp_gelu_kernel(
     nc = tc.nc
     with ExitStack() as ctx:
         keep = ctx.enter_context(tc.tile_pool(name="keep", bufs=1))
-        ring = ctx.enter_context(tc.tile_pool(name="ring", bufs=2))
         psum = ctx.enter_context(tc.psum_pool(name="psum", bufs=1))
 
         offsets = keep.tile([P, S // 16], U16, name="offsets")
         gate_sb = keep.tile([P, S], F32, name="gate_sb")
         x_rows = [[keep.tile([P, T], F32, name=f"x{s}_{t}") for t in range(PACK)] for s in range(PASSES)]
         w1 = [keep.tile([P, PASSES, 2 * H], U8, name=f"w1_{e}", align_bytes=64) for e in range(E)]
-        w2 = [keep.tile([P, 2 * N], U8, name=f"w2_{e}", align_bytes=64) for e in range(E)]
-        w1s = [keep.tile([P, 2, PASSES, H], U8, name=f"w1s_{g}", align_bytes=64) for g in range(2)]
+        w2 = keep.tile([P, E, 2 * N], U8, name="w2", align_bytes=64)
+        w1s = keep.tile([P, E * PASSES, H], U8, name="w1s", align_bytes=64)
         w2s = keep.tile([P, E, N], U8, name="w2s", align_bytes=64)
         ident = keep.tile([P, P], F32, name="ident")
         windows = [keep.tile([P, T], F32, name=f"win{j}") for j in range(N_TILES)]
-        x_bf = [keep.tile([P, S, PACK], BF16, name=f"xb{s}", align_bytes=64) for s in range(PASSES)]
+        stage = keep.tile([P, 8 * S], F32, name="stage")
         x_codes = [keep.tile([P, S], U32, name=f"xq{s}", align_bytes=64) for s in range(PASSES)]
         x_scales = [keep.tile([P, S], U8, name=f"xs{s}", align_bytes=64) for s in range(PASSES)]
-        h_slot = [keep.tile([P, H], BF16, name=f"hs{e}", align_bytes=64) for e in range(E)]
-        h_bf = [keep.tile([P, C * PACK], BF16, name=f"hb{e}", align_bytes=64) for e in range(E)]
-        h_codes = [keep.tile([P, C], U32, name=f"hq{e}", align_bytes=64) for e in range(E)]
-        h_scales = [keep.tile([P, C], U8, name=f"hsc{e}", align_bytes=64) for e in range(E)]
-        y_sb = keep.tile([P, N_TILES, S], F32, name="y_sb")
-        a_ps = [psum.tile([P, H], F32, name=f"a{e}") for e in range(E)]
+        h_codes = [keep.tile([P, G], U32, name=f"hq{g}", align_bytes=64) for g in range(2)]
+        h_scales = [keep.tile([P, G], U8, name=f"hsc{g}", align_bytes=64) for g in range(2)]
         t_ps = [psum.tile([P, 2, C], F32, name=f"t{j}") for j in range(2)]
-        y_ps = [psum.tile([P, N_TILES, C], F32, name=f"y{j}") for j in range(2)]
 
         def load_x(s, t):
             rows = xT[s * K_PASS : (s + 1) * K_PASS, :].rearrange("(p t) c -> t p c", t=PACK)
@@ -63,93 +58,106 @@ def tile_moe_pre_mlp_gelu_kernel(
         def load_w1(e):
             nc.sync.dma_start(out=w1[e][:].bitcast(I32), in_=w1_words[e].rearrange("s p b -> p s b").bitcast(I32))
 
-        def load_w2(e):
-            nc.sync.dma_start(out=w2[e][:].bitcast(I32), in_=w2_words[e, 0].bitcast(I32))
+        def load_w2(g):
+            nc.sync.dma_start(
+                out=w2[:, 2 * g : 2 * g + 2, :].bitcast(I32),
+                in_=w2_words[2 * g : 2 * g + 2].rearrange("e s p b -> p (e s) b").bitcast(I32),
+            )
 
-        def load_w1_scales(g):
-            src = w1_scales[2 * g : 2 * g + 2].rearrange("e s q i -> q (e s) i")
-            dst = w1s[g][:].rearrange("p e s i -> p (e s) i")
+        def load_scales(dst, src):
+            rows = src.rearrange("e s q i -> q (e s) i")
             for quad in range(4):
                 nc.sync.dma_start(
-                    out=dst[32 * quad : 32 * quad + 4].bitcast(I32), in_=src[4 * quad : 4 * quad + 4].bitcast(I32)
+                    out=dst[32 * quad : 32 * quad + 4].bitcast(I32), in_=rows[4 * quad : 4 * quad + 4].bitcast(I32)
                 )
 
-        def load_w2_scales():
-            src = w2_scales.rearrange("e s q n -> q (e s) n")
-            for quad in range(4):
-                nc.sync.dma_start(
-                    out=w2s[32 * quad : 32 * quad + 4].bitcast(I32), in_=src[4 * quad : 4 * quad + 4].bitcast(I32)
-                )
-
-        def gather(s, c0, c1):
-            gathered = ring.tile([P, PACK, c1 - c0], F32, name="gathered")
-            for t in range(PACK):
+        def gather(s, c0, c1, at, step, order=(0, 1, 2, 3)):
+            planes = stage[:, at : at + PACK * step].rearrange("p (t w) -> p t w", t=PACK)[:, :, 0 : c1 - c0]
+            for t in order:
                 nc.vector.tensor_tensor(
-                    gathered[:, t, :],
+                    planes[:, t, :],
                     x_rows[s][t][:].indirect(offsets[:, c0 // 16 : c1 // 16]),
                     gate_sb[:, c0:c1],
                     MULT,
                 )
-            nc.scalar.copy(
-                out=x_bf[s][:, c0:c1, :].rearrange("p (c i) t -> p c t i", i=4),
-                in_=gathered[:].rearrange("p t (c i) -> p c t i", i=4),
-            )
+            return planes
 
-        def quantize_x(s, c0, c1):
+        def interleave(planes, tag):
+            x_bf = keep.tile([P, planes.shape[2], PACK], BF16, name="x_bf", tag=tag, align_bytes=64)
+            nc.scalar.copy(
+                out=x_bf[:].rearrange("p (c i) t -> p c t i", i=4),
+                in_=planes.rearrange("p t (c i) -> p c t i", i=4),
+            )
+            return x_bf
+
+        def quantize_x(s, c0, c1, x_bf):
             nc.vector.quantize_mx(
                 out=x_codes[s][:, c0:c1].bitcast(FP8X4),
                 scales=x_scales[s][:, c0:c1],
-                in_=x_bf[s][:, c0:c1, :].rearrange("p c t -> p (c t)"),
+                in_=x_bf[:].rearrange("p c t -> p (c t)"),
             )
 
-        def layer1(e, s):
+        def layer1(acc, e, s):
             cols = slice(e * C, (e + 1) * C)
             nc.tensor.matmul_mx(
-                out=a_ps[e][:],
+                out=acc[:],
                 lhsT=x_codes[s][:, cols].bitcast(FP8X4),
                 lhsT_scale=x_scales[s][:, cols],
                 rhs=w1[e][:, s, :].bitcast(FP4X4),
-                rhs_scale=w1s[e // 2][:, e % 2, s, :],
+                rhs_scale=w1s[:, e * PASSES + s, :],
                 start=(s == 0),
                 stop=(s == PASSES - 1),
             )
 
-        def hidden(e):
+        def gelu(acc, h_slot):
             nc.scalar.activation(
-                out=h_slot[e][:].rearrange("c (u m d) -> c u m d", u=2, d=2),
-                in_=a_ps[e][:].rearrange("c (m u d) -> c u m d", u=2, d=2),
+                out=h_slot.rearrange("c (u m d) -> c u m d", u=2, d=2),
+                in_=acc[:].rearrange("c (m u d) -> c u m d", u=2, d=2),
                 func=GELU,
             )
-            words = h_slot[e][:].bitcast(F32)
-            tp = t_ps[e % 2]
+
+        def turn(h_slot, tp, h_bf):
+            words = h_slot.bitcast(F32)
             for u in range(2):
                 nc.tensor.transpose(tp[:, u, :], words[:, u * P : (u + 1) * P], ident[:])
             nc.scalar.copy(
-                out=h_bf[e][:].bitcast(F32).rearrange("p (c u) -> p c u", u=2),
+                out=h_bf.bitcast(F32).rearrange("p (c u) -> p c u", u=2),
                 in_=tp[:].rearrange("p u c -> p c u"),
             )
 
-        def layer2(e):
-            nc.vector.quantize_mx(out=h_codes[e][:].bitcast(FP8X4), scales=h_scales[e][:], in_=h_bf[e][:])
-            yp = y_ps[e % 2]
+        def hidden(g, accs, slot_tags, bf_tag):
+            h_slot = [keep.tile([P, H], BF16, name="h_slot", tag=tag, align_bytes=64) for tag in slot_tags]
+            h_bf = keep.tile([P, G * PACK], BF16, name="h_bf", tag=bf_tag, align_bytes=64)
+            for i in range(2):
+                gelu(accs[i], h_slot[i][:])
+            for i in range(2):
+                turn(h_slot[i][:], t_ps[i], h_bf[:, i * H : (i + 1) * H])
+            nc.vector.quantize_mx(out=h_codes[g][:].bitcast(FP8X4), scales=h_scales[g][:], in_=h_bf[:])
+
+        def layer2(g, tags):
+            banks = [psum.tile([P, 2, G], F32, name="y_ps", tag=tag) for tag in tags]
             for j in range(N_TILES):
-                nc.tensor.matmul_mx(
-                    out=yp[:, j, :],
-                    lhsT=w2[e][:, 2 * j * P : 2 * (j + 1) * P].bitcast(FP4X4),
-                    lhsT_scale=w2s[:, e, j * P : (j + 1) * P],
-                    rhs=h_codes[e][:].bitcast(FP8X4),
-                    rhs_scale=h_scales[e][:],
-                    start=True,
-                    stop=True,
-                )
-            nc.scalar.copy(out=y_sb[:, :, e * C : (e + 1) * C], in_=yp[:])
+                for i in range(2):
+                    e = 2 * g + i
+                    cols = slice(i * C, (i + 1) * C)
+                    nc.tensor.matmul_mx(
+                        out=banks[j // 2][:, j % 2, cols],
+                        lhsT=w2[:, e, 2 * j * P : 2 * (j + 1) * P].bitcast(FP4X4),
+                        lhsT_scale=w2s[:, e, j * P : (j + 1) * P],
+                        rhs=h_codes[g][:, cols].bitcast(FP8X4),
+                        rhs_scale=h_scales[g][:, cols],
+                        start=True,
+                        stop=True,
+                    )
+            return banks
 
-        def scatter(j, c0, c1):
-            nc.vector.tensor_copy(windows[j][:].indirect(offsets[:, c0 // 16 : c1 // 16]), y_sb[:, j, c0:c1])
+        def scatter(g, j, banks, tag):
+            y_sb = keep.tile([P, G], F32, name="y_sb", tag=tag, align_bytes=64)
+            nc.scalar.copy(out=y_sb[:], in_=banks[j // 2][:, j % 2, :])
+            nc.vector.tensor_copy(windows[j][:].indirect(offsets[:, g * G // 16 : (g + 1) * G // 16]), y_sb[:])
 
-        for g in range(2):
-            nc.vector.memset(w1s[g][:].rearrange("p e s i -> p (e s i)").bitcast(I32), 0)
-        nc.vector.memset(w2s[:].rearrange("p e n -> p (e n)").bitcast(I32), 0)
+        nc.gpsimd.memset(w1s[:].rearrange("p a i -> p (a i)").bitcast(I32), 0)
+        nc.gpsimd.memset(w2s[:].rearrange("p e n -> p (e n)").bitcast(I32), 0)
         nc.vector.memset(windows[0][:], 0.0)
         for j in range(1, N_TILES):
             nc.scalar.activation(out=windows[j][:], in_=windows[0][:], func=GELU)
@@ -158,68 +166,53 @@ def tile_moe_pre_mlp_gelu_kernel(
         nc.sync.dma_start(offsets[:], offs)
         load_x(0, 0)
         nc.sync.dma_start(out=gate_sb[:], in_=gate[0:P, :])
-        for s in range(2):
+        for s in range(PASSES):
             for t in range(PACK):
                 if (s, t) != (0, 0):
                     load_x(s, t)
-        load_w1_scales(0)
-        for s in range(2, PASSES):
-            for t in range(PACK):
-                load_x(s, t)
+        load_scales(w1s, w1_scales)
+        load_scales(w2s, w2_scales)
         load_w1(0)
         load_w1(1)
-        load_w2_scales()
-        load_w1_scales(1)
         load_w2(0)
-        load_w2(1)
         load_w1(2)
         load_w1(3)
-        load_w2(2)
-        load_w2(3)
+        load_w2(1)
 
-        gather(0, 0, S)
-        gather(1, 0, S)
-        quantize_x(0, 0, S)
-        gather(2, 0, 2 * C)
-        quantize_x(1, 0, S)
-        gather(3, 0, C)
-        quantize_x(2, 0, 2 * C)
-        for s in range(3):
-            layer1(0, s)
-        gather(3, C, 2 * C)
-        quantize_x(3, 0, C)
-        layer1(0, 3)
-        hidden(0)
-        for s in range(3):
-            layer1(1, s)
-        gather(2, 2 * C, S)
-        quantize_x(3, C, 2 * C)
-        layer1(1, 3)
-        hidden(1)
-        gather(3, 2 * C, 3 * C)
-        layer2(0)
-        quantize_x(2, 2 * C, S)
-        for s in range(3):
-            layer1(2, s)
-        gather(3, 3 * C, S)
-        quantize_x(3, 2 * C, 3 * C)
-        layer1(2, 3)
-        hidden(2)
-        layer2(1)
-        for s in range(3):
-            layer1(3, s)
-        scatter(0, 0, C)
-        quantize_x(3, 3 * C, S)
-        layer1(3, 3)
-        hidden(3)
-        for j in range(1, N_TILES):
-            scatter(j, 0, C)
-        layer2(2)
+        accs = [psum.tile([P, H], F32, name="acc", tag=f"acc{e}") for e in range(E)]
+        xb0 = interleave(gather(0, 0, S, 2048, S), "xb0")
+        xb1 = interleave(gather(1, 0, S, 0, S), "xb1")
+        quantize_x(0, 0, S, xb0)
+        xb2a = interleave(gather(2, 0, G, 2048, G), "xb2a")
+        quantize_x(1, 0, S, xb1)
+        xb3a = interleave(gather(3, 0, G, 640, 384), "xb3a")
+        quantize_x(2, 0, G, xb2a)
+        for e in range(2):
+            for s in range(3):
+                layer1(accs[e], e, s)
+        quantize_x(3, 0, G, xb3a)
+        for e in range(2):
+            layer1(accs[e], e, 3)
+        planes2b = gather(2, G, S, 1536, G, order=(2, 3, 0, 1))
+        planes3b = gather(3, G, S, 512, G)
+        hidden(0, accs[0:2], ("slot0", "slot1"), "hbf0")
+        banks_a = layer2(0, ("ya0", "ya1"))
+        for e in range(2, 4):
+            for s in range(2):
+                layer1(accs[e], e, s)
+        xb2b = interleave(planes2b, "slot1")
+        quantize_x(2, G, S, xb2b)
+        for e in range(2, 4):
+            layer1(accs[e], e, 2)
+        xb3b = interleave(planes3b, "hbf0")
+        quantize_x(3, G, S, xb3b)
+        for e in range(2, 4):
+            layer1(accs[e], e, 3)
+        for j in range(3):
+            scatter(0, j, banks_a, f"ya{j}")
+        hidden(1, accs[2:4], ("slot2", "slot3"), "hbf1")
+        banks_b = layer2(1, ("acc0", "acc1"))
+        scatter(0, 3, banks_a, "slot3")
         for j in range(N_TILES):
-            scatter(j, C, 2 * C)
-        layer2(3)
-        for j in range(N_TILES):
-            scatter(j, 2 * C, 3 * C)
-        for j in range(N_TILES):
-            scatter(j, 3 * C, S)
+            scatter(1, j, banks_b, f"yb{j}")
             nc.sync.dma_start(out=out[j * P : (j + 1) * P, :], in_=windows[j][:])

@@ -36,19 +36,18 @@ def tile_moe_pre_mlp_gelu_kernel(
         psum = ctx.enter_context(tc.psum_pool(name="psum", bufs=1))
 
         offsets = keep.tile([P, S // 16], U16, name="offsets")
-        gate_sb = keep.tile([P, S], F32, name="gate_sb")
-        x_rows = [[keep.tile([P, T], F32, name=f"x{s}_{t}") for t in range(PACK)] for s in range(PASSES)]
+        gate_sb = keep.tile([P, S], F32, name="gate_sb", align_bytes=64)
+        gate_b = keep.tile([P, G], F32, name="gate_b")
+        x_rows = [[keep.tile([P, T], F32, name=f"x{s}_{t}", align_bytes=64) for t in range(PACK)] for s in range(PASSES)]
         w1 = [keep.tile([P, PASSES, 2 * H], U8, name=f"w1_{e}", align_bytes=64) for e in range(E)]
         w2 = keep.tile([P, E, 2 * N], U8, name="w2", align_bytes=64)
-        w1s = keep.tile([P, E * PASSES, H], U8, name="w1s", align_bytes=64)
+        w1s = [keep.tile([P, 2 * PASSES, H], U8, name=f"w1s{g}", align_bytes=64) for g in range(2)]
         w2s = keep.tile([P, E, N], U8, name="w2s", align_bytes=64)
         ident = keep.tile([P, P], F32, name="ident")
         windows = [keep.tile([P, T], F32, name=f"win{j}") for j in range(N_TILES)]
-        stage = keep.tile([P, 8 * S], F32, name="stage")
-        x_codes = [keep.tile([P, S], U32, name=f"xq{s}", align_bytes=64) for s in range(PASSES)]
+        stage = keep.tile([P, 2944], F32, name="stage", align_bytes=64)
         x_scales = [keep.tile([P, S], U8, name=f"xs{s}", align_bytes=64) for s in range(PASSES)]
-        h_codes = [keep.tile([P, G], U32, name=f"hq{g}", align_bytes=64) for g in range(2)]
-        h_scales = [keep.tile([P, G], U8, name=f"hsc{g}", align_bytes=64) for g in range(2)]
+        h_scales = keep.tile([P, S], U8, name="h_scales", align_bytes=64)
         t_ps = [psum.tile([P, 2, C], F32, name=f"t{j}") for j in range(2)]
 
         def load_x(s, t):
@@ -71,92 +70,94 @@ def tile_moe_pre_mlp_gelu_kernel(
                     out=dst[32 * quad : 32 * quad + 4].bitcast(I32), in_=rows[4 * quad : 4 * quad + 4].bitcast(I32)
                 )
 
-        def gather(s, c0, c1, at, step, order=(0, 1, 2, 3)):
-            planes = stage[:, at : at + PACK * step].rearrange("p (t w) -> p t w", t=PACK)[:, :, 0 : c1 - c0]
+        def planes_at(at, step):
+            return stage[:, at : at + PACK * step].rearrange("p (t w) -> p t w", t=PACK)[:, :, 0:G]
+
+        def gather(s, c0, c1, planes, gates, order):
             for t in order:
                 nc.vector.tensor_tensor(
-                    planes[:, t, :],
-                    x_rows[s][t][:].indirect(offsets[:, c0 // 16 : c1 // 16]),
-                    gate_sb[:, c0:c1],
-                    MULT,
+                    planes[:, t, :], x_rows[s][t][:].indirect(offsets[:, c0 // 16 : c1 // 16]), gates, MULT
                 )
-            return planes
 
-        def interleave(planes, tag):
-            x_bf = keep.tile([P, planes.shape[2], PACK], BF16, name="x_bf", tag=tag, align_bytes=64)
+        def bf_tile(width, tag):
+            t = keep.tile([P, width * PACK], BF16, name="bf", tag=tag, align_bytes=64)
+            return t[:]
+
+        def interleave(planes, x_bf):
             nc.scalar.copy(
-                out=x_bf[:].rearrange("p (c i) t -> p c t i", i=4),
+                out=x_bf.rearrange("p (c i t) -> p c t i", i=4, t=PACK),
                 in_=planes.rearrange("p t (c i) -> p c t i", i=4),
             )
             return x_bf
 
-        def quantize_x(s, c0, c1, x_bf):
-            nc.vector.quantize_mx(
-                out=x_codes[s][:, c0:c1].bitcast(FP8X4),
-                scales=x_scales[s][:, c0:c1],
-                in_=x_bf[:].rearrange("p c t -> p (c t)"),
-            )
+        def quantize(codes, scales, values):
+            nc.vector.quantize_mx(out=codes.bitcast(FP8X4), scales=scales, in_=values)
 
-        def layer1(acc, e, s):
-            cols = slice(e * C, (e + 1) * C)
+        codes = {}
+
+        def layer1(e, s, first, last):
             nc.tensor.matmul_mx(
-                out=acc[:],
-                lhsT=x_codes[s][:, cols].bitcast(FP8X4),
-                lhsT_scale=x_scales[s][:, cols],
+                out=accs[e][:],
+                lhsT=codes[s, e].bitcast(FP8X4),
+                lhsT_scale=x_scales[s][:, e * C : (e + 1) * C],
                 rhs=w1[e][:, s, :].bitcast(FP4X4),
-                rhs_scale=w1s[:, e * PASSES + s, :],
-                start=(s == 0),
-                stop=(s == PASSES - 1),
+                rhs_scale=w1s[e // 2][:, (e % 2) * PASSES + s, :],
+                start=(s == first),
+                stop=(s == last),
             )
 
-        def gelu(acc, h_slot):
+        def gelu(e):
+            h_slot = bf_tile(C, f"slot{e}")
             nc.scalar.activation(
                 out=h_slot.rearrange("c (u m d) -> c u m d", u=2, d=2),
-                in_=acc[:].rearrange("c (m u d) -> c u m d", u=2, d=2),
+                in_=accs[e][:].rearrange("c (m u d) -> c u m d", u=2, d=2),
                 func=GELU,
             )
+            return h_slot
 
-        def turn(h_slot, tp, h_bf):
+        def turn(e, h_slot):
             words = h_slot.bitcast(F32)
+            tp = t_ps[e % 2]
+            h_bf = bf_tile(C, f"hbf{e}")
             for u in range(2):
                 nc.tensor.transpose(tp[:, u, :], words[:, u * P : (u + 1) * P], ident[:])
             nc.scalar.copy(
                 out=h_bf.bitcast(F32).rearrange("p (c u) -> p c u", u=2),
                 in_=tp[:].rearrange("p u c -> p c u"),
             )
+            return h_bf
 
-        def hidden(g, accs, slot_tags, bf_tag):
-            h_slot = [keep.tile([P, H], BF16, name="h_slot", tag=tag, align_bytes=64) for tag in slot_tags]
-            h_bf = keep.tile([P, G * PACK], BF16, name="h_bf", tag=bf_tag, align_bytes=64)
-            for i in range(2):
-                gelu(accs[i], h_slot[i][:])
-            for i in range(2):
-                turn(h_slot[i][:], t_ps[i], h_bf[:, i * H : (i + 1) * H])
-            nc.vector.quantize_mx(out=h_codes[g][:].bitcast(FP8X4), scales=h_scales[g][:], in_=h_bf[:])
-
-        def layer2(g, tags):
-            banks = [psum.tile([P, 2, G], F32, name="y_ps", tag=tag) for tag in tags]
+        def layer2(e, h_bf, tag):
+            h_codes = keep.tile([P, C], U32, name="h_codes", tag=f"hq{e}", align_bytes=64)
+            scales = h_scales[:, e * C : (e + 1) * C]
+            quantize(h_codes[:], scales, h_bf)
+            bank = psum.tile([P, N_TILES, C], F32, name="y_ps", tag=tag)
             for j in range(N_TILES):
-                for i in range(2):
-                    e = 2 * g + i
-                    cols = slice(i * C, (i + 1) * C)
-                    nc.tensor.matmul_mx(
-                        out=banks[j // 2][:, j % 2, cols],
-                        lhsT=w2[:, e, 2 * j * P : 2 * (j + 1) * P].bitcast(FP4X4),
-                        lhsT_scale=w2s[:, e, j * P : (j + 1) * P],
-                        rhs=h_codes[g][:, cols].bitcast(FP8X4),
-                        rhs_scale=h_scales[g][:, cols],
-                        start=True,
-                        stop=True,
-                    )
-            return banks
+                nc.tensor.matmul_mx(
+                    out=bank[:, j, :],
+                    lhsT=w2[:, e, 2 * j * P : 2 * (j + 1) * P].bitcast(FP4X4),
+                    lhsT_scale=w2s[:, e, j * P : (j + 1) * P],
+                    rhs=h_codes[:].bitcast(FP8X4),
+                    rhs_scale=scales,
+                    start=True,
+                    stop=True,
+                )
+            y_ps[e] = bank
 
-        def scatter(g, j, banks, tag):
-            y_sb = keep.tile([P, G], F32, name="y_sb", tag=tag, align_bytes=64)
-            nc.scalar.copy(out=y_sb[:], in_=banks[j // 2][:, j % 2, :])
-            nc.vector.tensor_copy(windows[j][:].indirect(offsets[:, g * G // 16 : (g + 1) * G // 16]), y_sb[:])
+        def y_tile(width, tag):
+            t = keep.tile([P, width], F32, name="y_sb", tag=tag, align_bytes=64)
+            return t[:]
 
-        nc.gpsimd.memset(w1s[:].rearrange("p a i -> p (a i)").bitcast(I32), 0)
+        def scatter(e0, e1, j, y_sb):
+            for e in range(e0, e1):
+                nc.scalar.copy(out=y_sb[:, (e - e0) * C : (e - e0 + 1) * C], in_=y_ps[e][:, j, :])
+            nc.vector.tensor_copy(windows[j][:].indirect(offsets[:, e0 * C // 16 : e1 * C // 16]), y_sb)
+
+        def store(j):
+            nc.sync.dma_start(out=out[j * P : (j + 1) * P, :], in_=windows[j][:])
+
+        for g in range(2):
+            nc.gpsimd.memset(w1s[g][:].rearrange("p a i -> p (a i)").bitcast(I32), 0)
         nc.gpsimd.memset(w2s[:].rearrange("p e n -> p (e n)").bitcast(I32), 0)
         nc.vector.memset(windows[0][:], 0.0)
         for j in range(1, N_TILES):
@@ -166,53 +167,92 @@ def tile_moe_pre_mlp_gelu_kernel(
         nc.sync.dma_start(offsets[:], offs)
         load_x(0, 0)
         nc.sync.dma_start(out=gate_sb[:], in_=gate[0:P, :])
-        for s in range(PASSES):
+        for s in (0, 2, 1, 3):
+            if s == 3:
+                load_scales(w1s[0], w1_scales[0:2])
             for t in range(PACK):
                 if (s, t) != (0, 0):
                     load_x(s, t)
-        load_scales(w1s, w1_scales)
-        load_scales(w2s, w2_scales)
+        nc.sync.dma_start(out=gate_b[:], in_=gate[0:P, G:S])
         load_w1(0)
         load_w1(1)
+        load_scales(w2s, w2_scales)
+        load_scales(w1s[1], w1_scales[2:4])
         load_w2(0)
-        load_w1(2)
         load_w1(3)
+        load_w1(2)
         load_w2(1)
 
         accs = [psum.tile([P, H], F32, name="acc", tag=f"acc{e}") for e in range(E)]
-        xb0 = interleave(gather(0, 0, S, 2048, S), "xb0")
-        xb1 = interleave(gather(1, 0, S, 0, S), "xb1")
-        quantize_x(0, 0, S, xb0)
-        xb2a = interleave(gather(2, 0, G, 2048, G), "xb2a")
-        quantize_x(1, 0, S, xb1)
-        xb3a = interleave(gather(3, 0, G, 640, 384), "xb3a")
-        quantize_x(2, 0, G, xb2a)
+        y_ps = {}
+        every = (0, 1, 2, 3)
+        g0 = keep.tile([P, PACK, S], F32, name="g0")
+        g2a = keep.tile([P, PACK, G], F32, name="g2a")
+        g1 = keep.tile([P, PACK, S], F32, name="g1")
+        g2b, g3a, g3b = planes_at(896, G), planes_at(1280, 416), planes_at(1792, G)
+        gather(0, 0, S, g0[:], gate_sb[:], every)
+        xb0 = interleave(g0[:], bf_tile(S, "xb0"))
+        gather(2, 0, G, g2a[:], gate_sb[:, 0:G], every)
+        xb2a = interleave(g2a[:], bf_tile(G, "xb2a"))
+        gather(1, 0, S, g1[:], gate_sb[:], every)
+        xb1 = interleave(g1[:], stage[:, 0:1024].bitcast(BF16))
+        early = keep.tile([P, S + G], U32, name="early", tag="x1_0", align_bytes=64)
+        quantize(early[:, 0:S], x_scales[0][:], xb0)
+        quantize(early[:, S : S + G], x_scales[2][:, 0:G], xb2a)
+        gather(3, 0, G, g3a, gate_sb[:, 0:G], every)
+        codes1 = keep.tile([P, S], U32, name="codes1", tag="gate_sb", align_bytes=64)
+        late = keep.tile([P, G + S], U32, name="late", align_bytes=64)
+        for e in range(E):
+            codes[0, e] = early[:, e * C : (e + 1) * C]
+            codes[1, e] = codes1[:, e * C : (e + 1) * C]
+            codes[2, e] = early[:, S + e * C : S + (e + 1) * C] if e < 2 else late[:, (e - 2) * C : (e - 1) * C]
+            codes[3, e] = late[:, G + e * C : G + (e + 1) * C]
+        quantize(codes1[:], x_scales[1][:], xb1)
         for e in range(2):
-            for s in range(3):
-                layer1(accs[e], e, s)
-        quantize_x(3, 0, G, xb3a)
+            for s in (0, 2):
+                layer1(e, s, 0, 3)
+
+        def half(planes, s, e, tag):
+            i = e % 2
+            xb = interleave(planes[:, :, i * C : (i + 1) * C], bf_tile(C, tag))
+            quantize(codes[s, e], x_scales[s][:, e * C : (e + 1) * C], xb)
+
         for e in range(2):
-            layer1(accs[e], e, 3)
-        planes2b = gather(2, G, S, 1536, G, order=(2, 3, 0, 1))
-        planes3b = gather(3, G, S, 512, G)
-        hidden(0, accs[0:2], ("slot0", "slot1"), "hbf0")
-        banks_a = layer2(0, ("ya0", "ya1"))
-        for e in range(2, 4):
-            for s in range(2):
-                layer1(accs[e], e, s)
-        xb2b = interleave(planes2b, "slot1")
-        quantize_x(2, G, S, xb2b)
-        for e in range(2, 4):
-            layer1(accs[e], e, 2)
-        xb3b = interleave(planes3b, "hbf0")
-        quantize_x(3, G, S, xb3b)
-        for e in range(2, 4):
-            layer1(accs[e], e, 3)
-        for j in range(3):
-            scatter(0, j, banks_a, f"ya{j}")
-        hidden(1, accs[2:4], ("slot2", "slot3"), "hbf1")
-        banks_b = layer2(1, ("acc0", "acc1"))
-        scatter(0, 3, banks_a, "slot3")
-        for j in range(N_TILES):
-            scatter(1, j, banks_b, f"yb{j}")
-            nc.sync.dma_start(out=out[j * P : (j + 1) * P, :], in_=windows[j][:])
+            half(g3a, 3, e, f"xb3{e}")
+            layer1(e, 1, 0, 3)
+            layer1(e, 3, 0, 3)
+        gather(2, G, S, g2b, gate_b[:], every)
+        gather(3, G, S, g3b, gate_b[:], (1, 2, 3))
+        slot0 = gelu(0)
+        slot1 = gelu(1)
+        layer2(0, turn(0, slot0), "y0")
+        half(g2b, 2, 3, "slot0")
+        gather(3, G, S, g3b, gate_b[:], (0,))
+        layer2(1, turn(1, slot1), "y1")
+        half(g2b, 2, 2, "slot1")
+        for s in (2, 0, 1):
+            layer1(3, s, 2, 3)
+        scatter(0, 1, 0, y_tile(C, "y00"))
+        half(g3b, 3, 3, "hq0")
+        layer1(3, 3, 2, 3)
+        scatter(0, 1, 1, stage[:, 2688:2816])
+        for s in (2, 0, 1):
+            layer1(2, s, 2, 3)
+        half(g3b, 3, 2, "hq1")
+        layer1(2, 3, 2, 3)
+        scatter(1, 2, 0, stage[:, 1792:1920])
+        scatter(1, 2, 1, y_tile(C, "y11"))
+        scatter(0, 2, 2, y_tile(G, "ya2"))
+        slot3 = gelu(3)
+        slot2 = gelu(2)
+        layer2(3, turn(3, slot3), "acc0")
+        scatter(0, 2, 3, y_tile(G, "slot3"))
+        layer2(2, turn(2, slot2), "acc1")
+        scatter(3, 4, 0, y_tile(C, "slot2"))
+        scatter(3, 4, 1, y_tile(C, "y31"))
+        for j in range(2):
+            scatter(2, 3, j, y_tile(C, f"y2{j}"))
+            store(j)
+        for j in range(2, 4):
+            scatter(2, 4, j, y_tile(G, f"yb{j}"))
+            store(j)

@@ -156,25 +156,25 @@ def tile_moe_pre_mlp_gelu_kernel(
         def store(j):
             nc.sync.dma_start(out=out[j * P : (j + 1) * P, :], in_=windows[j][:])
 
-        for g in range(2):
-            nc.gpsimd.memset(w1s[g][:].rearrange("p a i -> p (a i)").bitcast(I32), 0)
-        nc.gpsimd.memset(w2s[:].rearrange("p e n -> p (e n)").bitcast(I32), 0)
         nc.vector.memset(windows[0][:], 0.0)
+        for g in range(2):
+            nc.vector.memset(w1s[g][:].rearrange("p a i -> p (a i)").bitcast(I32), 0)
+        nc.vector.memset(w2s[:].rearrange("p e n -> p (e n)").bitcast(I32), 0)
         for j in range(1, N_TILES):
             nc.scalar.activation(out=windows[j][:], in_=windows[0][:], func=GELU)
         make_identity(nc, ident[:])
 
         nc.sync.dma_start(offsets[:], offs)
         load_x(0, 0)
-        nc.sync.dma_start(out=gate_sb[:], in_=gate[0:P, :])
+        nc.sync.dma_start(out=gate_sb[:, 0:G], in_=gate[0:P, 0:G])
+        nc.sync.dma_start(out=gate_sb[:, G:S], in_=gate[0:P, G:S])
         for s in (0, 2, 1, 3):
-            if s == 3:
-                load_scales(w1s[0], w1_scales[0:2])
             for t in range(PACK):
                 if (s, t) != (0, 0):
                     load_x(s, t)
-        nc.sync.dma_start(out=gate_b[:], in_=gate[0:P, G:S])
+        load_scales(w1s[0], w1_scales[0:2])
         load_w1(0)
+        nc.sync.dma_start(out=gate_b[:], in_=gate[0:P, G:S])
         load_w1(1)
         load_scales(w2s, w2_scales)
         load_scales(w1s[1], w1_scales[2:4])
@@ -190,7 +190,9 @@ def tile_moe_pre_mlp_gelu_kernel(
         g2a = keep.tile([P, PACK, G], F32, name="g2a")
         g1 = keep.tile([P, PACK, S], F32, name="g1")
         g2b, g3a, g3b = planes_at(896, G), planes_at(1280, 416), planes_at(1792, G)
-        gather(0, 0, S, g0[:], gate_sb[:], every)
+        gather(0, 0, G, g0[:, :, 0:G], gate_sb[:, 0:G], (0,))
+        gather(0, G, S, g0[:, :, G:S], gate_sb[:, G:S], (0,))
+        gather(0, 0, S, g0[:], gate_sb[:], (1, 2, 3))
         xb0 = interleave(g0[:], bf_tile(S, "xb0"))
         gather(2, 0, G, g2a[:], gate_sb[:, 0:G], every)
         xb2a = interleave(g2a[:], bf_tile(G, "xb2a"))

from contextlib import ExitStack

import concourse.mybir as mybir
from concourse.masks import make_identity

K, T, E, C, H, N = 2048, 640, 4, 128, 512, 512
S = E * C
G = 2 * C
P = 128
PACK = 4
K_PASS = P * PACK
PASSES = K // K_PASS
N_TILES = N // P

FLOPS = 2 * S * (K * H + H * N)
BYTES = 4 * K * T + E * (K * H + H * N) // 2 + E * (K * H + H * N) // 32 + 4 * P * S + 2 * P * S // 16 + 4 * N * T

F32 = mybir.dt.float32
BF16 = mybir.dt.bfloat16
I32 = mybir.dt.int32
U32 = mybir.dt.uint32
U16 = mybir.dt.uint16
U8 = mybir.dt.uint8
FP8X4 = mybir.dt.float8_e4m3fn_x4
FP4X4 = mybir.dt.float4_e2m1fn_x4
MULT = mybir.AluOpType.mult
GELU = mybir.ActivationFunctionType.Gelu_apprx_tanh


def tile_moe_pre_mlp_gelu_kernel(
    tc, xT, w1_words, w1_scales, w2_words, w2_scales, gate, offs, out
):
    nc = tc.nc
    with ExitStack() as ctx:
        keep = ctx.enter_context(tc.tile_pool(name="keep", bufs=1))
        psum = ctx.enter_context(tc.psum_pool(name="psum", bufs=1))

        offsets = keep.tile([P, S // 16], U16, name="offsets")
        gate_sb = keep.tile([P, S], F32, name="gate_sb", align_bytes=64)
        gate_b = keep.tile([P, G], F32, name="gate_b")
        x_rows = [[keep.tile([P, T], F32, name=f"x{s}_{t}", align_bytes=64) for t in range(PACK)] for s in range(PASSES)]
        w1 = [keep.tile([P, PASSES, 2 * H], U8, name=f"w1_{e}", align_bytes=64) for e in range(E)]
        w2 = keep.tile([P, E, 2 * N], U8, name="w2", align_bytes=64)
        w1s = [keep.tile([P, 2 * PASSES, H], U8, name=f"w1s{g}", align_bytes=64) for g in range(2)]
        w2s = keep.tile([P, E, N], U8, name="w2s", align_bytes=64)
        ident = keep.tile([P, P], F32, name="ident")
        windows = [keep.tile([P, T], F32, name=f"win{j}") for j in range(N_TILES)]
        stage = keep.tile([P, 2944], F32, name="stage", align_bytes=64)
        x_scales = [keep.tile([P, S], U8, name=f"xs{s}", align_bytes=64) for s in range(PASSES)]
        h_scales = keep.tile([P, S], U8, name="h_scales", align_bytes=64)
        t_ps = [psum.tile([P, 2, C], F32, name=f"t{j}") for j in range(2)]

        def load_x(s, t):
            rows = xT[s * K_PASS : (s + 1) * K_PASS, :].rearrange("(p t) c -> t p c", t=PACK)
            nc.sync.dma_start(out=x_rows[s][t][:], in_=rows[t])

        def load_w1(e):
            nc.sync.dma_start(out=w1[e][:].bitcast(I32), in_=w1_words[e].rearrange("s p b -> p s b").bitcast(I32))

        def load_w2(g):
            nc.sync.dma_start(
                out=w2[:, 2 * g : 2 * g + 2, :].bitcast(I32),
                in_=w2_words[2 * g : 2 * g + 2].rearrange("e s p b -> p (e s) b").bitcast(I32),
            )

        def load_scales(dst, src):
            rows = src.rearrange("e s q i -> q (e s) i")
            for quad in range(4):
                nc.sync.dma_start(
                    out=dst[32 * quad : 32 * quad + 4].bitcast(I32), in_=rows[4 * quad : 4 * quad + 4].bitcast(I32)
                )

        def planes_at(at, step):
            return stage[:, at : at + PACK * step].rearrange("p (t w) -> p t w", t=PACK)[:, :, 0:G]

        def gather(s, c0, c1, planes, gates, order):
            for t in order:
                nc.vector.tensor_tensor(
                    planes[:, t, :], x_rows[s][t][:].indirect(offsets[:, c0 // 16 : c1 // 16]), gates, MULT
                )

        def bf_tile(width, tag):
            t = keep.tile([P, width * PACK], BF16, name="bf", tag=tag, align_bytes=64)
            return t[:]

        def interleave(planes, x_bf):
            nc.scalar.copy(
                out=x_bf.rearrange("p (c i t) -> p c t i", i=4, t=PACK),
                in_=planes.rearrange("p t (c i) -> p c t i", i=4),
            )
            return x_bf

        def quantize(codes, scales, values):
            nc.vector.quantize_mx(out=codes.bitcast(FP8X4), scales=scales, in_=values)

        codes = {}

        def layer1(e, s, first, last):
            nc.tensor.matmul_mx(
                out=accs[e][:],
                lhsT=codes[s, e].bitcast(FP8X4),
                lhsT_scale=x_scales[s][:, e * C : (e + 1) * C],
                rhs=w1[e][:, s, :].bitcast(FP4X4),
                rhs_scale=w1s[e // 2][:, (e % 2) * PASSES + s, :],
                start=(s == first),
                stop=(s == last),
            )

        def gelu(e):
            h_slot = bf_tile(C, f"slot{e}")
            nc.scalar.activation(
                out=h_slot.rearrange("c (u m d) -> c u m d", u=2, d=2),
                in_=accs[e][:].rearrange("c (m u d) -> c u m d", u=2, d=2),
                func=GELU,
            )
            return h_slot

        def turn(e, h_slot):
            words = h_slot.bitcast(F32)
            tp = t_ps[e % 2]
            h_bf = bf_tile(C, f"hbf{e}")
            for u in range(2):
                nc.tensor.transpose(tp[:, u, :], words[:, u * P : (u + 1) * P], ident[:])
            nc.scalar.copy(
                out=h_bf.bitcast(F32).rearrange("p (c u) -> p c u", u=2),
                in_=tp[:].rearrange("p u c -> p c u"),
            )
            return h_bf

        def layer2(e, h_bf, tag):
            h_codes = keep.tile([P, C], U32, name="h_codes", tag=f"hq{e}", align_bytes=64)
            scales = h_scales[:, e * C : (e + 1) * C]
            quantize(h_codes[:], scales, h_bf)
            bank = psum.tile([P, N_TILES, C], F32, name="y_ps", tag=tag)
            for j in range(N_TILES):
                nc.tensor.matmul_mx(
                    out=bank[:, j, :],
                    lhsT=w2[:, e, 2 * j * P : 2 * (j + 1) * P].bitcast(FP4X4),
                    lhsT_scale=w2s[:, e, j * P : (j + 1) * P],
                    rhs=h_codes[:].bitcast(FP8X4),
                    rhs_scale=scales,
                    start=True,
                    stop=True,
                )
            y_ps[e] = bank

        def y_tile(width, tag):
            t = keep.tile([P, width], F32, name="y_sb", tag=tag, align_bytes=64)
            return t[:]

        def scatter(e0, e1, j, y_sb):
            for e in range(e0, e1):
                nc.scalar.copy(out=y_sb[:, (e - e0) * C : (e - e0 + 1) * C], in_=y_ps[e][:, j, :])
            nc.vector.tensor_copy(windows[j][:].indirect(offsets[:, e0 * C // 16 : e1 * C // 16]), y_sb)

        def store(j):
            nc.sync.dma_start(out=out[j * P : (j + 1) * P, :], in_=windows[j][:])

        nc.vector.memset(windows[0][:], 0.0)
        for g in range(2):
            nc.vector.memset(w1s[g][:].rearrange("p a i -> p (a i)").bitcast(I32), 0)
        nc.vector.memset(w2s[:].rearrange("p e n -> p (e n)").bitcast(I32), 0)
        for j in range(1, N_TILES):
            nc.scalar.activation(out=windows[j][:], in_=windows[0][:], func=GELU)
        make_identity(nc, ident[:])

        nc.sync.dma_start(offsets[:], offs)
        load_x(0, 0)
        nc.sync.dma_start(out=gate_sb[:, 0:G], in_=gate[0:P, 0:G])
        nc.sync.dma_start(out=gate_sb[:, G:S], in_=gate[0:P, G:S])
        for s in (0, 2, 1, 3):
            for t in range(PACK):
                if (s, t) != (0, 0):
                    load_x(s, t)
        load_scales(w1s[0], w1_scales[0:2])
        load_w1(0)
        nc.sync.dma_start(out=gate_b[:], in_=gate[0:P, G:S])
        load_w1(1)
        load_scales(w2s, w2_scales)
        load_scales(w1s[1], w1_scales[2:4])
        load_w2(0)
        load_w1(3)
        load_w1(2)
        load_w2(1)

        accs = [psum.tile([P, H], F32, name="acc", tag=f"acc{e}") for e in range(E)]
        y_ps = {}
        every = (0, 1, 2, 3)
        g0 = keep.tile([P, PACK, S], F32, name="g0")
        g2a = keep.tile([P, PACK, G], F32, name="g2a")
        g1 = keep.tile([P, PACK, S], F32, name="g1")
        g2b, g3a, g3b = planes_at(896, G), planes_at(1280, 416), planes_at(1792, G)
        gather(0, 0, G, g0[:, :, 0:G], gate_sb[:, 0:G], (0,))
        gather(0, G, S, g0[:, :, G:S], gate_sb[:, G:S], (0,))
        gather(0, 0, S, g0[:], gate_sb[:], (1, 2, 3))
        xb0 = interleave(g0[:], bf_tile(S, "xb0"))
        gather(2, 0, G, g2a[:], gate_sb[:, 0:G], every)
        xb2a = interleave(g2a[:], bf_tile(G, "xb2a"))
        gather(1, 0, S, g1[:], gate_sb[:], every)
        xb1 = interleave(g1[:], stage[:, 0:1024].bitcast(BF16))
        early = keep.tile([P, S + G], U32, name="early", tag="x1_0", align_bytes=64)
        quantize(early[:, 0:S], x_scales[0][:], xb0)
        quantize(early[:, S : S + G], x_scales[2][:, 0:G], xb2a)
        gather(3, 0, G, g3a, gate_sb[:, 0:G], every)
        codes1 = keep.tile([P, S], U32, name="codes1", tag="gate_sb", align_bytes=64)
        late = keep.tile([P, G + S], U32, name="late", align_bytes=64)
        for e in range(E):
            codes[0, e] = early[:, e * C : (e + 1) * C]
            codes[1, e] = codes1[:, e * C : (e + 1) * C]
            codes[2, e] = early[:, S + e * C : S + (e + 1) * C] if e < 2 else late[:, (e - 2) * C : (e - 1) * C]
            codes[3, e] = late[:, G + e * C : G + (e + 1) * C]
        quantize(codes1[:], x_scales[1][:], xb1)
        for e in range(2):
            for s in (0, 2):
                layer1(e, s, 0, 3)

        def half(planes, s, e, tag):
            i = e % 2
            xb = interleave(planes[:, :, i * C : (i + 1) * C], bf_tile(C, tag))
            quantize(codes[s, e], x_scales[s][:, e * C : (e + 1) * C], xb)

        for e in range(2):
            half(g3a, 3, e, f"xb3{e}")
            layer1(e, 1, 0, 3)
            layer1(e, 3, 0, 3)
        gather(2, G, S, g2b, gate_b[:], every)
        gather(3, G, S, g3b, gate_b[:], (1, 2, 3))
        slot0 = gelu(0)
        slot1 = gelu(1)
        layer2(0, turn(0, slot0), "y0")
        half(g2b, 2, 3, "slot0")
        gather(3, G, S, g3b, gate_b[:], (0,))
        layer2(1, turn(1, slot1), "y1")
        half(g2b, 2, 2, "slot1")
        for s in (2, 0, 1):
            layer1(3, s, 2, 3)
        scatter(0, 1, 0, y_tile(C, "y00"))
        half(g3b, 3, 3, "hq0")
        layer1(3, 3, 2, 3)
        scatter(0, 1, 1, stage[:, 2688:2816])
        for s in (2, 0, 1):
            layer1(2, s, 2, 3)
        half(g3b, 3, 2, "hq1")
        layer1(2, 3, 2, 3)
        scatter(1, 2, 0, stage[:, 1792:1920])
        scatter(1, 2, 1, y_tile(C, "y11"))
        scatter(0, 2, 2, y_tile(G, "ya2"))
        slot3 = gelu(3)
        slot2 = gelu(2)
        layer2(3, turn(3, slot3), "acc0")
        scatter(0, 2, 3, y_tile(G, "slot3"))
        layer2(2, turn(2, slot2), "acc1")
        scatter(3, 4, 0, y_tile(C, "slot2"))
        scatter(3, 4, 1, y_tile(C, "y31"))
        for j in range(2):
            scatter(2, 3, j, y_tile(C, f"y2{j}"))
            store(j)
        for j in range(2, 4):
            scatter(2, 4, j, y_tile(G, f"yb{j}"))
            store(j)
